import numpy as np
import ml_dtypes


def mxq(x, axis, fmt="e4m3"):
    dtype, down = {"e4m3": (ml_dtypes.float8_e4m3fn, 7), "e5m2": (ml_dtypes.float8_e5m2, 14)}[fmt]
    v = np.moveaxis(np.asarray(x, np.float32).astype(ml_dtypes.bfloat16).astype(np.float64), axis, -1)
    blocks = v.reshape(v.shape[:-1] + (-1, 32))
    amax = np.abs(blocks).max(-1, keepdims=True)
    byte = np.maximum(np.where(amax > 0, np.frexp(amax)[1] - 1 + 127, 0) - down, 1)
    scale = np.exp2(byte - 127.0)
    codes = (blocks / scale).astype(np.float32).astype(dtype).astype(np.float64)
    return np.moveaxis((codes * scale).reshape(v.shape), -1, axis)


WIDE = False


def mx_kscale(k):
    if not WIDE:
        return np.ones(k)
    levels = np.array([10, -10, 5, -5, 0])
    if k % 512:
        return np.exp2(np.random.permutation(np.resize(levels, k // 32))).repeat(32)
    a = np.empty((k // 512, 16))
    for p in range(k // 512):
        a[p, :8] = np.random.permutation(np.resize(levels, 8))
        for g in range(8):
            far = levels[np.abs(levels - a[p, g]) >= 10]
            a[p, g + 8] = far[np.random.randint(len(far))]
    return np.exp2(a.ravel()).repeat(32)


BF16 = ml_dtypes.bfloat16


def bf(x):
    return np.asarray(x, np.float32).astype(BF16)


def f64(x):
    return np.asarray(x).astype(np.float64)


E2M1 = np.array([0.0, 0.5, 1.0, 1.5, 2.0, 3.0, 4.0, 6.0, -0.0, -0.5, -1.0, -1.5, -2.0, -3.0, -4.0, -6.0])


def pack_weight(w, fmt):
    k, n = w.shape
    w = f64(bf(w)).reshape(k // 32, 32, n)
    amax = np.abs(w).max(1)
    if fmt == "e4m3":
        byte = np.frexp(amax)[1] - 1 + 127 - 7
    else:
        mant, ex = np.frexp(amax / 6.0)
        byte = np.where(mant > 0.5, ex, ex - 1) + 127
    byte = np.clip(np.where(amax > 0, byte, 1), 1, 254)
    scaled = (w * np.exp2(127.0 - byte)[:, None, :]).reshape(k, n).astype(np.float32)
    by_word = np.ascontiguousarray(scaled.reshape(k // 512, 128, 4, n).transpose(0, 1, 3, 2))
    if fmt == "e4m3":
        words = by_word.astype(ml_dtypes.float8_e4m3fn).view(np.uint8)
    else:
        c = by_word.astype(ml_dtypes.float4_e2m1fn).view(np.uint8) & 0xF
        words = c[..., 0::2] | (c[..., 1::2] << 4)
    return np.ascontiguousarray(words), np.ascontiguousarray(byte.astype(np.uint8).reshape(k // 512, 16, n))


def unpack_weight(words, scales, fmt):
    g, p, n, _ = words.shape
    if fmt == "e4m3":
        vals = np.ascontiguousarray(words).view(ml_dtypes.float8_e4m3fn).astype(np.float64)
    else:
        nib = np.empty((g, p, n, 4), np.uint8)
        nib[..., 0::2] = words & 0xF
        nib[..., 1::2] = words >> 4
        vals = E2M1[nib]
    vals = vals * np.repeat(np.exp2(scales.astype(np.float64) - 127.0), 8, axis=1)[..., None]
    return vals.transpose(0, 1, 3, 2).reshape(g * 512, n)

def planes(Y):
    n, m = Y.shape
    b = f64(bf(Y)).reshape(n // 32, 32, m)
    amax = np.abs(b).max(1)
    byte = np.clip(np.where(amax > 0, np.frexp(amax)[1] - 1 + 127 - 7, 1), 1, 254)
    codes = (b * np.exp2(127.0 - byte)[:, None, :]).reshape(n, m).astype(np.float32).astype(ml_dtypes.float8_e4m3fn).view(np.uint8)
    words = codes.reshape(n // 512, 128, 4, m).transpose(0, 1, 3, 2)
    return np.ascontiguousarray(words), np.ascontiguousarray(byte.astype(np.uint8).reshape(n // 512, 16, m))


N, D, M, V = 512, 1024, 2048, 2048


def row_logsumexp(x):
    top = np.max(x, axis=-1, keepdims=True)
    return top + np.log(np.sum(np.exp(x - top), axis=-1, keepdims=True))


def row_softmax(x):
    top = np.max(x, axis=-1, keepdims=True)
    ex = np.exp(x - top)
    return ex / np.sum(ex, axis=-1, keepdims=True)


def sigmoid(v):
    return 1.0 / (1.0 + np.exp(-v))


def setup_inputs():
    s, t = mx_kscale(D), mx_kscale(M)
    h = bf(np.random.standard_normal((N, D)) * s)
    keys = np.random.standard_normal((M, D)) * (32.0 / np.sqrt(D)) / s
    kb = bf(np.random.standard_normal(M))
    g = bf(np.random.standard_normal(M) * t)
    val = np.random.standard_normal((M, V)) * (np.sqrt(M) / 45.0) / t[:, None]
    w_lm = np.random.standard_normal((D, V)) / np.sqrt(D) / s[:, None]
    keys_words, keys_scales = pack_weight(keys.T, "e4m3")
    val_words, val_scales = pack_weight(val, "e4m3")
    w_lm_words, w_lm_scales = pack_weight(w_lm, "e4m3")
    return {
        "h": h,
        "keys_words": keys_words,
        "keys_scales": keys_scales,
        "kb": kb,
        "g": g,
        "val_words": val_words,
        "val_scales": val_scales,
        "w_lm_words": w_lm_words,
        "w_lm_scales": w_lm_scales,
    }


def core(h, keys_words, keys_scales, kb, g, val_words, val_scales, w_lm_words, w_lm_scales):
    vocab = w_lm_words.shape[2]
    hq = mxq(f64(h), 1, "e4m3")

    e = (hq @ unpack_weight(keys_words, keys_scales, "e4m3")) / 20.0 + f64(kb)[None, :]

    l = row_logsumexp(e)
    w = np.exp(e - l)

    a = 8.0 * w * f64(g)[None, :]

    knn = mxq(a, 1, "e4m3") @ unpack_weight(val_words, val_scales, "e4m3")

    z = hq @ unpack_weight(w_lm_words, w_lm_scales, "e4m3")
    p_lm = row_softmax(z)

    lam = sigmoid(4.0 * (l - np.mean(l)))

    return lam * knn + (1.0 - lam) * (vocab * p_lm - 1.0)


def reference(h, keys_words, keys_scales, kb, g, val_words, val_scales, w_lm_words, w_lm_scales):
    R_out = core(h, keys_words, keys_scales, kb, g, val_words, val_scales, w_lm_words, w_lm_scales)
    words, scales = planes(R_out)
    return R_out, words, scales

@@ -1,0 +1,521 @@
+from contextlib import ExitStack
+
+import concourse.mybir as mybir
+from concourse.masks import make_identity
+
+N, D, M, V = 512, 1024, 2048, 2048
+FLOPS = 2 * N * (D * M + D * V + M * V)
+
+F32 = mybir.dt.float32
+BF16 = mybir.dt.bfloat16
+U32 = mybir.dt.uint32
+I32 = mybir.dt.int32
+U8 = mybir.dt.uint8
+FP8X4 = mybir.dt.float8_e4m3fn_x4
+ACT = mybir.ActivationFunctionType
+OP = mybir.AluOpType
+AX = mybir.AxisListType
+
+P = 128
+T = 4
+C = 512
+NC = 4
+
+
+def tile_gatedmemoryattentionlmhead_kernel(
+    tc, h, keys_words, keys_scales, kb, g, val_words, val_scales, w_lm_words, w_lm_scales, out_0, out_1, out_2
+):
+    nc = tc.nc
+    with ExitStack() as ctx:
+        keep = ctx.enter_context(tc.tile_pool(name="keep", bufs=1))
+        work = ctx.enter_context(tc.tile_pool(name="work", bufs=2))
+        acc = ctx.enter_context(tc.psum_pool(name="acc", bufs=6))
+        trp = ctx.enter_context(tc.psum_pool(name="trp", bufs=2))
+        ctx.enter_context(tc.manual_schedule())
+
+        h_sb = keep.tile([P, 2, 2, D], BF16, name="h_sb")
+        h_gr = keep.tile([P, 2, 2, 2 * P, 4], BF16, name="h_gr", align_bytes=64)
+        hq = keep.tile([P, 2, 2, 2 * P], U32, name="hq", align_bytes=64)
+        hqs = keep.tile([P, 2, 2, 2 * P], U8, name="hqs", align_bytes=64)
+        k_w = [keep.tile([P, 2, C], U32, name="k_w%d" % c, align_bytes=64) for c in range(NC)]
+        w_w = [keep.tile([P, 2, C], U32, name="w_w%d" % c, align_bytes=64) for c in range(NC)]
+        v_w = [keep.tile([P, 4, C], U32, name="v_w%d" % c, align_bytes=64) for c in range(NC)]
+        k_sc = keep.tile([P, M], U8, name="k_sc", align_bytes=64)
+        w_sc = keep.tile([P, V], U8, name="w_sc", align_bytes=64)
+        v_sc = keep.tile([P, V], U8, name="v_sc", align_bytes=64)
+        kb_row = keep.tile([P, M], BF16, name="kb_row")
+        g_row = keep.tile([P, M], BF16, name="g_row")
+        kb_b = keep.tile([P, M], BF16, name="kb_b")
+        g_b = keep.tile([P, M], BF16, name="g_b")
+        ones = keep.tile([P, P], BF16, name="ones")
+        eights = keep.tile([P, P], BF16, name="eights")
+        mean_w = keep.tile([P, P], F32, name="mean_w")
+        ident = keep.tile([P, P], F32, name="ident")
+        aq = [keep.tile([P, 4, P], U32, name="aq%d" % t, align_bytes=64) for t in range(T)]
+        aqs = [keep.tile([P, 4, P], U8, name="aqs%d" % t, align_bytes=64) for t in range(T)]
+        y = keep.tile([P, T, V], F32, name="y")
+        oq = keep.tile([P, V], U32, name="oq", align_bytes=64)
+        oqs = keep.tile([P, V], U8, name="oqs", align_bytes=64)
+        junk = keep.tile([P, M], BF16, name="junk")
+        nm = keep.tile([P, T], F32, name="nm")
+        ssum = keep.tile([P, T], F32, name="ssum")
+        rs = keep.tile([P, T], F32, name="rs")
+        lns = keep.tile([P, T], F32, name="lns")
+        ell = keep.tile([P, T], F32, name="ell")
+        lsum = keep.tile([P, 1], F32, name="lsum")
+        b4 = keep.tile([P, 1], F32, name="b4")
+        ed = keep.tile([P, T], F32, name="ed")
+        den = keep.tile([P, T], F32, name="den")
+        lam = keep.tile([P, T], F32, name="lam")
+        c0 = keep.tile([P, T], F32, name="c0")
+        c1 = keep.tile([P, T], F32, name="c1")
+        zmx = keep.tile([P, T, NC], F32, name="zmx")
+        zj = keep.tile([P, NC], F32, name="zj")
+        znm = keep.tile([P, T], F32, name="znm")
+        zs4 = keep.tile([P, T, NC], F32, name="zs4")
+        zs = keep.tile([P, T], F32, name="zs")
+        rz = keep.tile([P, T], F32, name="rz")
+        warm = keep.tile([P, 1], F32, name="warm")
+
+        def cols(c):
+            return slice(c * C, (c + 1) * C)
+
+        h_v = h.rearrange("(p t) k -> p t k", t=T)
+
+        def load_scales(tile, src, n):
+            for q in range(4):
+                nc.sync.dma_start(
+                    out=tile[32 * q : 32 * q + 4 * n, :].bitcast(I32),
+                    in_=src[:, 4 * q : 4 * q + 4, :].bitcast(I32),
+                )
+
+        def load_words(tiles, src, c):
+            nc.sync.dma_start(
+                out=tiles[c][:].bitcast(I32),
+                in_=src[:, :, cols(c), :].rearrange("q p n t -> p q (n t)").bitcast(I32),
+            )
+
+        nc.sync.dma_start(out=h_sb[:, 0, :, :], in_=h_v[:, 0:2, :])
+        nc.vector.memset(kb_row[:], 0.0)
+        nc.vector.memset(k_sc[:].bitcast(I32), 0)
+        nc.vector.memset(w_sc[:].bitcast(I32), 0)
+        nc.vector.memset(v_sc[:].bitcast(I32), 0)
+        nc.vector.memset(ones[:], 1.0)
+        nc.vector.memset(eights[:], 8.0)
+        nc.vector.memset(mean_w[:], 4.0 / N)
+        nc.vector.memset(warm[:], 0.0)
+        make_identity(nc, ident[:])
+        nc.gpsimd.memset(g_row[:], 0.0)
+        nc.scalar.activation(out=warm[:], in_=warm[:], func=ACT.Exp)
+        nc.sync.dma_start(out=kb_row[0:1, :], in_=kb.rearrange("(o n) -> o n", o=1))
+        load_scales(k_sc, keys_scales, 2)
+        load_words(k_w, keys_words, 0)
+        for c in range(1, NC):
+            load_words(k_w, keys_words, c)
+        nc.sync.dma_start(out=h_sb[:, 1, :, :], in_=h_v[:, 2:4, :])
+        nc.sync.dma_start(out=g_row[0:1, :], in_=g.rearrange("(o n) -> o n", o=1))
+        load_scales(w_sc, w_lm_scales, 2)
+        for c in range(NC):
+            load_words(w_w, w_lm_words, c)
+        load_scales(v_sc, val_scales, 4)
+        for c in range(NC):
+            load_words(v_w, val_words, c)
+
+        h_words = h_gr[:].rearrange("p s q n j -> p (s q n j)").bitcast(F32)
+
+        h_ps = {}
+
+        def hturn(s2):
+            for q in range(2):
+                ps = trp.tile([P, 2, 2, P], F32, name="tr")
+                h_ps[(s2, q)] = ps
+                for i in range(2):
+                    wv = h_sb[:, s2, i, cols(q)].bitcast(F32)
+                    for u in range(2):
+                        nc.tensor.transpose(ps[:, i, u, :], wv[:, u : C // 2 : 2], ident[:])
+
+        def hcopy(s2, q):
+            lo = s2 * 1024 + q * 512
+            dst = h_words[:, lo : lo + 512].rearrange("p (i r u) -> p i r u", i=2, u=2)
+            src = h_ps[(s2, q)][:].rearrange("p i u r -> p i r u")
+            if q == 0:
+                nc.vector.tensor_copy(out=dst, in_=src)
+            else:
+                nc.scalar.copy(out=dst, in_=src)
+
+        def hquant(s2):
+            nc.vector.quantize_mx(
+                out=hq[:, s2, :, :].rearrange("p q n -> p (q n)").bitcast(FP8X4),
+                scales=hqs[:, s2, :, :].rearrange("p q n -> p (q n)"),
+                in_=h_gr[:, s2, :, :, :].rearrange("p q n j -> p (q n j)"),
+            )
+
+        sp_ps = {}
+
+        def spread_mm(key, lhs, row):
+            for half in range(2):
+                ps = acc.tile([P, 1024], BF16, name="ps")
+                sp_ps[(key, half)] = ps
+                for i in range(2):
+                    lo = half * 1024 + i * C
+                    nc.tensor.matmul(
+                        ps[:, i * C : (i + 1) * C], lhsT=lhs[:], rhs=row[:, lo : lo + C], start=True, stop=True
+                    )
+
+        def spread_copy(key, dst):
+            for half in range(2):
+                nc.scalar.copy(out=dst[:, half * 1024 : half * 1024 + 1024], in_=sp_ps[(key, half)][:])
+
+        s_t = {}
+        sb_t = {}
+        a_t = {}
+        ga_t = {}
+        z_ps = {}
+        k_ps = {}
+        ob_t = {}
+
+        def mx(ps, stat, stat_s, words, sc, c, n):
+            for q in range(n):
+                nc.tensor.matmul_mx(
+                    out=ps[:],
+                    lhsT=stat[q],
+                    lhsT_scale=stat_s[q],
+                    rhs=words[c][:, q, :].bitcast(FP8X4),
+                    rhs_scale=sc[4 * q : P, cols(c)],
+                    start=(q == 0),
+                    stop=(q == n - 1),
+                )
+
+        def hstat(t):
+            sl = slice((t % 2) * P, (t % 2 + 1) * P)
+            return [hq[:, t // 2, q, sl].bitcast(FP8X4) for q in range(2)], [hqs[:, t // 2, q, sl] for q in range(2)]
+
+        def score(t, c):
+            st, ss = hstat(t)
+            if t not in s_t:
+                s_t[t] = work.tile([P, M], F32, name="s", bufs=3)
+                sb_t[t] = work.tile([P, M], BF16, name="sb", bufs=2)
+            ps = acc.tile([P, C], F32, name="ps")
+            mx(ps, st, ss, k_w, k_sc, c, 2)
+            nc.vector.scalar_tensor_tensor(
+                out=s_t[t][:, cols(c)], in0=ps[:], scalar=1.0 / 20.0, in1=kb_b[:, cols(c)], op0=OP.mult, op1=OP.add
+            )
+            nc.gpsimd.tensor_scalar(
+                out=sb_t[t][:, cols(c)], in0=s_t[t][:, cols(c)], scalar1=1.0, scalar2=0.0, op0=OP.mult, op1=OP.add
+            )
+
+        def smax(t):
+            nc.vector.tensor_scalar(
+                out=junk[:], in0=sb_t[t][:], scalar1=-1.0, scalar2=None, op0=OP.mult, op1=OP.min, accum_out=nm[:, t : t + 1]
+            )
+
+        def sexp(t):
+            nc.scalar.activation(
+                out=s_t[t][:], in_=s_t[t][:], func=ACT.Exp, bias=nm[:, t : t + 1], accum_out=ssum[:, t : t + 1]
+            )
+
+        def srec(t):
+            nc.vector.reciprocal(out=rs[:, t : t + 1], in_=ssum[:, t : t + 1])
+
+        def gain(t):
+            a_t[t] = work.tile([P, M], BF16, name="a", bufs=2)
+            nc.vector.scalar_tensor_tensor(
+                out=a_t[t][:], in0=s_t[t][:], scalar=rs[:, t : t + 1], in1=g_b[:], op0=OP.mult, op1=OP.mult
+            )
+
+        tr_ps = {}
+
+        def turn(t):
+            av = a_t[t][:].bitcast(F32)
+            for half in range(2):
+                ps = trp.tile([P, 2, 2, P], F32, name="tr")
+                tr_ps[(t, half)] = ps
+                for i in range(2):
+                    q = 2 * half + i
+                    for u in range(2):
+                        nc.tensor.transpose(ps[:, i, u, :], av[:, 256 * q + u : 256 * (q + 1) : 2], ident[:])
+
+        def tcopy(t):
+            ga_t[t] = work.tile([P, 4, P, 4], BF16, name="ga", bufs=2, align_bytes=64)
+            dw = ga_t[t][:].rearrange("p q r j -> p (q r j)").bitcast(F32)
+            for half in range(2):
+                nc.scalar.copy(
+                    out=dw[:, half * 512 : half * 512 + 512].rearrange("p (i r u) -> p i r u", i=2, u=2),
+                    in_=tr_ps[(t, half)][:].rearrange("p i u r -> p i r u"),
+                )
+
+        def aquant(t):
+            nc.vector.quantize_mx(
+                out=aq[t][:].rearrange("p q r -> p (q r)").bitcast(FP8X4),
+                scales=aqs[t][:].rearrange("p q r -> p (q r)"),
+                in_=ga_t[t][:].rearrange("p q r j -> p (q r j)"),
+            )
+
+        def zmm(t):
+            st, ss = hstat(t)
+            z_ps[t] = []
+            for c in range(NC):
+                ps = acc.tile([P, C], F32, name="ps")
+                mx(ps, st, ss, w_w, w_sc, c, 2)
+                z_ps[t].append(ps)
+
+        def zmax(t, half):
+            for c in (2 * half, 2 * half + 1):
+                nc.vector.tensor_reduce(out=zmx[:, t, c : c + 1], in_=z_ps[t][c][:], axis=AX.X, op=OP.max)
+
+        def zneg(t):
+            nc.vector.tensor_scalar(
+                out=zj[:], in0=zmx[:, t, :], scalar1=-1.0, scalar2=None, op0=OP.mult, op1=OP.min, accum_out=znm[:, t : t + 1]
+            )
+
+        def zexp(t):
+            for c in range(NC):
+                nc.scalar.activation(
+                    out=y[:, t, cols(c)], in_=z_ps[t][c][:], func=ACT.Exp, bias=znm[:, t : t + 1],
+                    accum_out=zs4[:, t, c : c + 1],
+                )
+
+        def zsum(t):
+            nc.vector.tensor_reduce(out=zs[:, t : t + 1], in_=zs4[:, t, :], axis=AX.X, op=OP.add)
+
+        def zinv(t):
+            nc.vector.reciprocal(out=rz[:, t : t + 1], in_=zs[:, t : t + 1])
+
+        def zc1(t):
+            nc.vector.tensor_scalar(
+                out=c1[:, t : t + 1], in0=rz[:, t : t + 1], scalar1=c0[:, t : t + 1], scalar2=-float(V), op0=OP.mult, op1=OP.mult
+            )
+
+        gate_ps = []
+
+        def g1():
+            nc.scalar.activation(out=lns[:], in_=ssum[:], func=ACT.Ln)
+
+        def g2():
+            nc.vector.tensor_tensor(out=ell[:], in0=lns[:], in1=nm[:], op=OP.subtract)
+
+        def g2b():
+            nc.vector.tensor_reduce(out=lsum[:], in_=ell[:], axis=AX.X, op=OP.add)
+
+        def g3():
+            ps = acc.tile([P, C], F32, name="ps")
+            nc.tensor.matmul(ps[:, 0:1], lhsT=mean_w[:], rhs=lsum[:], start=True, stop=True)
+            gate_ps.append(ps)
+
+        def g4():
+            nc.vector.tensor_copy(out=b4[:], in_=gate_ps[0][:, 0:1])
+
+        def g5():
+            nc.scalar.activation(out=ed[:], in_=ell[:], func=ACT.Exp, bias=b4[:], scale=-4.0)
+
+        def g6():
+            nc.vector.tensor_scalar(out=den[:], in0=ed[:], scalar1=1.0, scalar2=None, op0=OP.add)
+
+        def g6b():
+            nc.vector.reciprocal(out=lam[:], in_=den[:])
+
+        def g7():
+            nc.vector.tensor_scalar(out=c0[:], in0=lam[:], scalar1=-1.0, scalar2=None, op0=OP.add)
+
+        def yaff(t):
+            for c in range(NC):
+                nc.gpsimd.tensor_scalar(
+                    out=y[:, t, cols(c)], in0=y[:, t, cols(c)], scalar1=c1[:, t : t + 1], scalar2=c0[:, t : t + 1],
+                    op0=OP.mult, op1=OP.add,
+                )
+
+        def kmm(t, c):
+            ps = acc.tile([P, C], F32, name="ps")
+            st = [aq[t][:, q, :].bitcast(FP8X4) for q in range(4)]
+            ss = [aqs[t][:, q, :] for q in range(4)]
+            mx(ps, st, ss, v_w, v_sc, c, 4)
+            k_ps[(t, c)] = ps
+
+        o_v = out_0.rearrange("(p t) m -> p t m", t=T)
+
+        def mix(t, c):
+            nc.vector.scalar_tensor_tensor(
+                out=y[:, t, cols(c)], in0=k_ps[(t, c)][:], scalar=lam[:, t : t + 1], in1=y[:, t, cols(c)], op0=OP.mult, op1=OP.add
+            )
+
+        def plane_copy(c, shares):
+            ob_t[c] = work.tile([P, C, 4], BF16, name="ob", bufs=2, align_bytes=64)
+            lo = 0
+            for eng, n in shares:
+                dst = ob_t[c][:, lo : lo + n, :]
+                src = y[:, :, c * C + lo : c * C + lo + n].rearrange("p t m -> p m t")
+                if eng == "S":
+                    nc.scalar.copy(out=dst, in_=src)
+                else:
+                    nc.vector.tensor_copy(out=dst, in_=src)
+                lo += n
+
+        def plane_quant(c):
+            nc.vector.quantize_mx(
+                out=oq[:, cols(c)].bitcast(FP8X4), scales=oqs[:, cols(c)], in_=ob_t[c][:].rearrange("p m j -> p (m j)")
+            )
+            nc.sync.dma_start(
+                out=out_1[0, :, cols(c), :].rearrange("p n t -> p (n t)").bitcast(I32), in_=oq[:, cols(c)].bitcast(I32)
+            )
+
+        hturn(0)
+        hcopy(0, 0)
+        hcopy(0, 1)
+        spread_mm("kb", ones, kb_row)
+        spread_copy("kb", kb_b)
+        hquant(0)
+        score(0, 0)
+        score(1, 0)
+        score(1, 1)
+        score(0, 1)
+        score(0, 2)
+        score(1, 2)
+        score(0, 3)
+        score(1, 3)
+        hturn(1)
+        spread_mm("g", eights, g_row)
+        hcopy(1, 0)
+        hcopy(1, 1)
+        smax(0)
+        hquant(1)
+        spread_copy("g", g_b)
+        sexp(0)
+        smax(1)
+        score(2, 1)
+        score(2, 0)
+        score(2, 3)
+        srec(0)
+        score(2, 2)
+        sexp(1)
+        gain(0)
+        smax(2)
+        score(3, 3)
+        score(3, 0)
+        score(3, 2)
+        sexp(2)
+        score(3, 1)
+        zmm(0)
+        zmax(0, 0)
+        smax(3)
+        srec(2)
+        turn(0)
+        srec(1)
+        tcopy(0)
+        sexp(3)
+        zmax(0, 1)
+        zneg(0)
+        g1()
+        gain(1)
+        zexp(0)
+        srec(3)
+        aquant(0)
+        gain(2)
+        g2()
+        turn(1)
+        zmm(1)
+        zmax(1, 0)
+        g2b()
+        zmax(1, 1)
+        zneg(1)
+        tcopy(1)
+        kmm(0, 1)
+        g3()
+        g4()
+        zsum(0)
+        g5()
+        aquant(1)
+        turn(2)
+        g6()
+        zexp(1)
+        kmm(0, 2)
+        kmm(0, 3)
+        zinv(0)
+        g6b()
+        g7()
+        zc1(0)
+        yaff(0)
+        gain(3)
+        mix(0, 1)
+        nc.sync.dma_start(out=o_v[:, 0, cols(1)], in_=y[:, 0, cols(1)])
+        zsum(1)
+        kmm(1, 2)
+        mix(0, 3)
+        nc.sync.dma_start(out=o_v[:, 0, cols(3)], in_=y[:, 0, cols(3)])
+        mix(0, 2)
+        nc.sync.dma_start(out=o_v[:, 0, cols(2)], in_=y[:, 0, cols(2)])
+        zmm(2)
+        zinv(1)
+        zc1(1)
+        tcopy(2)
+        turn(3)
+        zmax(2, 0)
+        zmax(2, 1)
+        tcopy(3)
+        kmm(1, 3)
+        yaff(1)
+        zneg(2)
+        mix(1, 2)
+        nc.sync.dma_start(out=o_v[:, 1, cols(2)], in_=y[:, 1, cols(2)])
+        zexp(2)
+        aquant(3)
+        mix(1, 3)
+        nc.sync.dma_start(out=o_v[:, 1, cols(3)], in_=y[:, 1, cols(3)])
+        zmm(3)
+        zmax(3, 0)
+        kmm(0, 0)
+        zmax(3, 1)
+        zsum(2)
+        zneg(3)
+        aquant(2)
+        zinv(2)
+        kmm(1, 1)
+        zexp(3)
+        kmm(1, 0)
+        zc1(2)
+        kmm(2, 0)
+        kmm(2, 3)
+        kmm(3, 0)
+        mix(0, 0)
+        nc.sync.dma_start(out=o_v[:, 0, cols(0)], in_=y[:, 0, cols(0)])
+        zsum(3)
+        yaff(2)
+        zinv(3)
+        zc1(3)
+        kmm(2, 2)
+        mix(1, 0)
+        nc.sync.dma_start(out=o_v[:, 1, cols(0)], in_=y[:, 1, cols(0)])
+        mix(1, 1)
+        nc.sync.dma_start(out=o_v[:, 1, cols(1)], in_=y[:, 1, cols(1)])
+        kmm(3, 2)
+        mix(2, 3)
+        nc.sync.dma_start(out=o_v[:, 2, cols(3)], in_=y[:, 2, cols(3)])
+        mix(2, 0)
+        nc.sync.dma_start(out=o_v[:, 2, cols(0)], in_=y[:, 2, cols(0)])
+        yaff(3)
+        mix(3, 0)
+        nc.sync.dma_start(out=o_v[:, 3, cols(0)], in_=y[:, 3, cols(0)])
+        kmm(3, 1)
+        plane_copy(0, [("S", 256), ("V", 256)])
+        mix(2, 2)
+        nc.sync.dma_start(out=o_v[:, 2, cols(2)], in_=y[:, 2, cols(2)])
+        plane_quant(0)
+        kmm(3, 3)
+        mix(3, 2)
+        nc.sync.dma_start(out=o_v[:, 3, cols(2)], in_=y[:, 3, cols(2)])
+        kmm(2, 1)
+        plane_copy(2, [("S", 256), ("V", 256)])
+        mix(3, 1)
+        nc.sync.dma_start(out=o_v[:, 3, cols(1)], in_=y[:, 3, cols(1)])
+        mix(3, 3)
+        nc.sync.dma_start(out=o_v[:, 3, cols(3)], in_=y[:, 3, cols(3)])
+        plane_quant(2)
+        mix(2, 1)
+        nc.sync.dma_start(out=o_v[:, 2, cols(1)], in_=y[:, 2, cols(1)])
+        plane_copy(3, [("S", 256), ("V", 256)])
+        plane_copy(1, [("S", 256), ("V", 256)])
+        plane_quant(3)
+        plane_quant(1)
+        for q in range(4):
+            nc.sync.dma_start(
+                out=out_2[0, 4 * q : 4 * q + 4, :].bitcast(I32), in_=oqs[32 * q : 32 * q + 4, :].bitcast(I32)
+            )

@@ -21,6 +21,10 @@ T = 4
 C = 512
 NC = 4
 
+DOWN = "SSNN"
+YENG = "SSSV"
+EVAC = "0000"
+
 
 def tile_gatedmemoryattentionlmhead_kernel(
     tc, h, keys_words, keys_scales, kb, g, val_words, val_scales, w_lm_words, w_lm_scales, out_0, out_1, out_2
@@ -172,6 +176,7 @@ def tile_gatedmemoryattentionlmhead_kernel(
         ga_t = {}
         z_ps = {}
         k_ps = {}
+        kc_t = {}
         ob_t = {}
 
         def mx(ps, stat, stat_s, words, sc, c, n):
@@ -193,20 +198,27 @@ def tile_gatedmemoryattentionlmhead_kernel(
         def score(t, c):
             st, ss = hstat(t)
             if t not in s_t:
-                s_t[t] = work.tile([P, M], F32, name="s", bufs=3)
-                sb_t[t] = work.tile([P, M], BF16, name="sb", bufs=2)
+                s_t[t] = work.tile([P, M], F32, name="s", bufs=4)
+                if DOWN[t] != "N":
+                    sb_t[t] = work.tile([P, M], BF16, name="sb", bufs=2)
             ps = acc.tile([P, C], F32, name="ps")
             mx(ps, st, ss, k_w, k_sc, c, 2)
             nc.vector.scalar_tensor_tensor(
                 out=s_t[t][:, cols(c)], in0=ps[:], scalar=1.0 / 20.0, in1=kb_b[:, cols(c)], op0=OP.mult, op1=OP.add
             )
-            nc.gpsimd.tensor_scalar(
-                out=sb_t[t][:, cols(c)], in0=s_t[t][:, cols(c)], scalar1=1.0, scalar2=0.0, op0=OP.mult, op1=OP.add
-            )
+            if DOWN[t] == "G":
+                nc.gpsimd.tensor_scalar(
+                    out=sb_t[t][:, cols(c)], in0=s_t[t][:, cols(c)], scalar1=1.0, scalar2=0.0, op0=OP.mult, op1=OP.add
+                )
+
+        def down(t, half):
+            sl = slice(half * 1024, half * 1024 + 1024)
+            nc.scalar.copy(out=sb_t[t][:, sl], in_=s_t[t][:, sl])
 
         def smax(t):
             nc.vector.tensor_scalar(
-                out=junk[:], in0=sb_t[t][:], scalar1=-1.0, scalar2=None, op0=OP.mult, op1=OP.min, accum_out=nm[:, t : t + 1]
+                out=junk[:], in0=(s_t if DOWN[t] == "N" else sb_t)[t][:], scalar1=-1.0, scalar2=None, op0=OP.mult, op1=OP.min,
+                accum_out=nm[:, t : t + 1],
             )
 
         def sexp(t):
@@ -217,32 +229,33 @@ def tile_gatedmemoryattentionlmhead_kernel(
         def srec(t):
             nc.vector.reciprocal(out=rs[:, t : t + 1], in_=ssum[:, t : t + 1])
 
-        def gain(t):
-            a_t[t] = work.tile([P, M], BF16, name="a", bufs=2)
+        def gain(t, half):
+            if t not in a_t:
+                a_t[t] = work.tile([P, M], BF16, name="a", bufs=2)
+            sl = slice(half * 1024, half * 1024 + 1024)
             nc.vector.scalar_tensor_tensor(
-                out=a_t[t][:], in0=s_t[t][:], scalar=rs[:, t : t + 1], in1=g_b[:], op0=OP.mult, op1=OP.mult
+                out=a_t[t][:, sl], in0=s_t[t][:, sl], scalar=rs[:, t : t + 1], in1=g_b[:, sl], op0=OP.mult, op1=OP.mult
             )
 
         tr_ps = {}
 
-        def turn(t):
+        def turn(t, half):
             av = a_t[t][:].bitcast(F32)
-            for half in range(2):
-                ps = trp.tile([P, 2, 2, P], F32, name="tr")
-                tr_ps[(t, half)] = ps
-                for i in range(2):
-                    q = 2 * half + i
-                    for u in range(2):
-                        nc.tensor.transpose(ps[:, i, u, :], av[:, 256 * q + u : 256 * (q + 1) : 2], ident[:])
+            ps = trp.tile([P, 2, 2, P], F32, name="tr")
+            tr_ps[(t, half)] = ps
+            for i in range(2):
+                q = 2 * half + i
+                for u in range(2):
+                    nc.tensor.transpose(ps[:, i, u, :], av[:, 256 * q + u : 256 * (q + 1) : 2], ident[:])
 
-        def tcopy(t):
-            ga_t[t] = work.tile([P, 4, P, 4], BF16, name="ga", bufs=2, align_bytes=64)
+        def tcopy(t, half):
+            if t not in ga_t:
+                ga_t[t] = work.tile([P, 4, P, 4], BF16, name="ga", bufs=2, align_bytes=64)
             dw = ga_t[t][:].rearrange("p q r j -> p (q r j)").bitcast(F32)
-            for half in range(2):
-                nc.scalar.copy(
-                    out=dw[:, half * 512 : half * 512 + 512].rearrange("p (i r u) -> p i r u", i=2, u=2),
-                    in_=tr_ps[(t, half)][:].rearrange("p i u r -> p i r u"),
-                )
+            nc.scalar.copy(
+                out=dw[:, half * 512 : half * 512 + 512].rearrange("p (i r u) -> p i r u", i=2, u=2),
+                in_=tr_ps[(t, half)][:].rearrange("p i u r -> p i r u"),
+            )
 
         def aquant(t):
             nc.vector.quantize_mx(
@@ -292,10 +305,9 @@ def tile_gatedmemoryattentionlmhead_kernel(
             nc.scalar.activation(out=lns[:], in_=ssum[:], func=ACT.Ln)
 
         def g2():
-            nc.vector.tensor_tensor(out=ell[:], in0=lns[:], in1=nm[:], op=OP.subtract)
-
-        def g2b():
-            nc.vector.tensor_reduce(out=lsum[:], in_=ell[:], axis=AX.X, op=OP.add)
+            nc.vector.scalar_tensor_tensor(
+                out=ell[:], in0=lns[:], scalar=1.0, in1=nm[:], op0=OP.mult, op1=OP.subtract, accum_out=lsum[:]
+            )
 
         def g3():
             ps = acc.tile([P, C], F32, name="ps")
@@ -319,7 +331,12 @@ def tile_gatedmemoryattentionlmhead_kernel(
 
         def yaff(t):
             for c in range(NC):
-                nc.gpsimd.tensor_scalar(
+                if YENG[t] == "S":
+                    nc.scalar.activation(
+                        out=y[:, t, cols(c)], in_=y[:, t, cols(c)], func=ACT.Identity, bias=c0[:, t : t + 1], scale=c1[:, t : t + 1]
+                    )
+                    continue
+                (nc.vector if YENG[t] == "V" else nc.gpsimd).tensor_scalar(
                     out=y[:, t, cols(c)], in0=y[:, t, cols(c)], scalar1=c1[:, t : t + 1], scalar2=c0[:, t : t + 1],
                     op0=OP.mult, op1=OP.add,
                 )
@@ -331,11 +348,16 @@ def tile_gatedmemoryattentionlmhead_kernel(
             mx(ps, st, ss, v_w, v_sc, c, 4)
             k_ps[(t, c)] = ps
 
+        def evac(t, c):
+            if t not in kc_t:
+                kc_t[t] = work.tile([P, V], F32, name="s", bufs=4)
+            nc.scalar.copy(out=kc_t[t][:, cols(c)], in_=k_ps[(t, c)][:])
+
         o_v = out_0.rearrange("(p t) m -> p t m", t=T)
 
         def mix(t, c):
             nc.vector.scalar_tensor_tensor(
-                out=y[:, t, cols(c)], in0=k_ps[(t, c)][:], scalar=lam[:, t : t + 1], in1=y[:, t, cols(c)], op0=OP.mult, op1=OP.add
+                out=y[:, t, cols(c)], in0=kc_t[t][:, cols(c)] if EVAC[t] == "1" else k_ps[(t, c)][:], scalar=lam[:, t : t + 1], in1=y[:, t, cols(c)], op0=OP.mult, op1=OP.add
             )
 
         def plane_copy(c, shares):
@@ -369,152 +391,167 @@ def tile_gatedmemoryattentionlmhead_kernel(
         score(1, 1)
         score(0, 1)
         score(0, 2)
+        down(1, 0)
+        down(0, 0)
         score(1, 2)
         score(0, 3)
         score(1, 3)
         hturn(1)
-        spread_mm("g", eights, g_row)
+        down(0, 1)
         hcopy(1, 0)
         hcopy(1, 1)
+        down(1, 1)
         smax(0)
+        spread_mm("g", eights, g_row)
         hquant(1)
-        spread_copy("g", g_b)
-        sexp(0)
         smax(1)
-        score(2, 1)
-        score(2, 0)
-        score(2, 3)
-        srec(0)
-        score(2, 2)
-        sexp(1)
-        gain(0)
-        smax(2)
-        score(3, 3)
-        score(3, 0)
-        score(3, 2)
-        sexp(2)
         score(3, 1)
+        score(3, 0)
+        spread_copy("g", g_b)
+        score(2, 3)
+        score(2, 1)
+        score(3, 3)
+        score(3, 2)
         zmm(0)
         zmax(0, 0)
-        smax(3)
-        srec(2)
-        turn(0)
-        srec(1)
-        tcopy(0)
-        sexp(3)
         zmax(0, 1)
+        score(2, 0)
+        sexp(0)
         zneg(0)
-        g1()
-        gain(1)
+        score(2, 2)
+        smax(3)
+        sexp(1)
         zexp(0)
-        srec(3)
-        aquant(0)
-        gain(2)
-        g2()
-        turn(1)
         zmm(1)
-        zmax(1, 0)
-        g2b()
-        zmax(1, 1)
-        zneg(1)
-        tcopy(1)
-        kmm(0, 1)
-        g3()
-        g4()
+        sexp(3)
+        smax(2)
+        srec(0)
         zsum(0)
-        g5()
-        aquant(1)
-        turn(2)
-        g6()
-        zexp(1)
-        kmm(0, 2)
-        kmm(0, 3)
+        gain(0, 0)
+        zmax(1, 0)
+        sexp(2)
+        zmax(1, 1)
         zinv(0)
+        turn(0, 0)
+        tcopy(0, 0)
+        srec(1)
+        zneg(1)
+        g1()
+        gain(0, 1)
+        turn(0, 1)
+        g2()
+        zexp(1)
+        g3()
+        zmm(2)
+        gain(1, 0)
+        gain(1, 1)
+        zmax(2, 0)
+        g4()
+        zmax(2, 1)
+        tcopy(0, 1)
+        g5()
+        turn(1, 0)
+        g6()
+        zneg(2)
+        zexp(2)
+        turn(1, 1)
+        aquant(0)
+        zmm(3)
         g6b()
+        srec(3)
+        kmm(0, 2)
+        zmax(3, 0)
         g7()
+        zmax(3, 1)
+        tcopy(1, 1)
+        tcopy(1, 0)
+        zsum(1)
+        zsum(2)
+        kmm(0, 1)
+        zneg(3)
+        zinv(1)
+        gain(3, 1)
+        aquant(1)
+        zexp(3)
+        kmm(0, 0)
+        srec(2)
         zc1(0)
+        kmm(1, 2)
         yaff(0)
-        gain(3)
+        gain(3, 0)
+        zsum(3)
+        gain(2, 0)
+        zc1(1)
+        turn(3, 1)
+        gain(2, 1)
+        tcopy(3, 1)
+        turn(3, 0)
         mix(0, 1)
         nc.sync.dma_start(out=o_v[:, 0, cols(1)], in_=y[:, 0, cols(1)])
-        zsum(1)
-        kmm(1, 2)
-        mix(0, 3)
-        nc.sync.dma_start(out=o_v[:, 0, cols(3)], in_=y[:, 0, cols(3)])
-        mix(0, 2)
-        nc.sync.dma_start(out=o_v[:, 0, cols(2)], in_=y[:, 0, cols(2)])
-        zmm(2)
-        zinv(1)
-        zc1(1)
-        tcopy(2)
-        turn(3)
-        zmax(2, 0)
-        zmax(2, 1)
-        tcopy(3)
-        kmm(1, 3)
-        yaff(1)
-        zneg(2)
-        mix(1, 2)
-        nc.sync.dma_start(out=o_v[:, 1, cols(2)], in_=y[:, 1, cols(2)])
-        zexp(2)
-        aquant(3)
-        mix(1, 3)
-        nc.sync.dma_start(out=o_v[:, 1, cols(3)], in_=y[:, 1, cols(3)])
-        zmm(3)
-        zmax(3, 0)
-        kmm(0, 0)
-        zmax(3, 1)
-        zsum(2)
-        zneg(3)
-        aquant(2)
         zinv(2)
-        kmm(1, 1)
-        zexp(3)
-        kmm(1, 0)
-        zc1(2)
-        kmm(2, 0)
-        kmm(2, 3)
-        kmm(3, 0)
+        kmm(0, 3)
+        turn(2, 0)
         mix(0, 0)
         nc.sync.dma_start(out=o_v[:, 0, cols(0)], in_=y[:, 0, cols(0)])
-        zsum(3)
-        yaff(2)
+        tcopy(3, 0)
+        turn(2, 1)
+        zc1(2)
+        mix(0, 2)
+        nc.sync.dma_start(out=o_v[:, 0, cols(2)], in_=y[:, 0, cols(2)])
+        tcopy(2, 0)
+        tcopy(2, 1)
         zinv(3)
+        yaff(1)
+        aquant(3)
         zc1(3)
-        kmm(2, 2)
-        mix(1, 0)
-        nc.sync.dma_start(out=o_v[:, 1, cols(0)], in_=y[:, 1, cols(0)])
+        kmm(1, 3)
+        aquant(2)
+        yaff(3)
+        kmm(1, 1)
         mix(1, 1)
         nc.sync.dma_start(out=o_v[:, 1, cols(1)], in_=y[:, 1, cols(1)])
-        kmm(3, 2)
-        mix(2, 3)
-        nc.sync.dma_start(out=o_v[:, 2, cols(3)], in_=y[:, 2, cols(3)])
-        mix(2, 0)
-        nc.sync.dma_start(out=o_v[:, 2, cols(0)], in_=y[:, 2, cols(0)])
-        yaff(3)
-        mix(3, 0)
-        nc.sync.dma_start(out=o_v[:, 3, cols(0)], in_=y[:, 3, cols(0)])
         kmm(3, 1)
-        plane_copy(0, [("S", 256), ("V", 256)])
-        mix(2, 2)
-        nc.sync.dma_start(out=o_v[:, 2, cols(2)], in_=y[:, 2, cols(2)])
-        plane_quant(0)
-        kmm(3, 3)
-        mix(3, 2)
-        nc.sync.dma_start(out=o_v[:, 3, cols(2)], in_=y[:, 3, cols(2)])
+        yaff(2)
+        mix(1, 2)
+        nc.sync.dma_start(out=o_v[:, 1, cols(2)], in_=y[:, 1, cols(2)])
         kmm(2, 1)
-        plane_copy(2, [("S", 256), ("V", 256)])
+        kmm(3, 2)
         mix(3, 1)
         nc.sync.dma_start(out=o_v[:, 3, cols(1)], in_=y[:, 3, cols(1)])
-        mix(3, 3)
-        nc.sync.dma_start(out=o_v[:, 3, cols(3)], in_=y[:, 3, cols(3)])
-        plane_quant(2)
+        mix(0, 3)
+        nc.sync.dma_start(out=o_v[:, 0, cols(3)], in_=y[:, 0, cols(3)])
+        mix(1, 3)
+        nc.sync.dma_start(out=o_v[:, 1, cols(3)], in_=y[:, 1, cols(3)])
+        kmm(2, 2)
         mix(2, 1)
         nc.sync.dma_start(out=o_v[:, 2, cols(1)], in_=y[:, 2, cols(1)])
-        plane_copy(3, [("S", 256), ("V", 256)])
+        kmm(3, 3)
+        kmm(2, 3)
+        mix(3, 2)
+        nc.sync.dma_start(out=o_v[:, 3, cols(2)], in_=y[:, 3, cols(2)])
         plane_copy(1, [("S", 256), ("V", 256)])
-        plane_quant(3)
+        kmm(3, 0)
+        mix(2, 2)
+        nc.sync.dma_start(out=o_v[:, 2, cols(2)], in_=y[:, 2, cols(2)])
         plane_quant(1)
+        kmm(1, 0)
+        plane_copy(2, [("S", 256), ("V", 256)])
+        mix(3, 3)
+        nc.sync.dma_start(out=o_v[:, 3, cols(3)], in_=y[:, 3, cols(3)])
+        mix(2, 3)
+        nc.sync.dma_start(out=o_v[:, 2, cols(3)], in_=y[:, 2, cols(3)])
+        kmm(2, 0)
+        plane_quant(2)
+        mix(3, 0)
+        nc.sync.dma_start(out=o_v[:, 3, cols(0)], in_=y[:, 3, cols(0)])
+        plane_copy(3, [("S", 256), ("V", 256)])
+        mix(1, 0)
+        nc.sync.dma_start(out=o_v[:, 1, cols(0)], in_=y[:, 1, cols(0)])
+        mix(2, 0)
+        nc.sync.dma_start(out=o_v[:, 2, cols(0)], in_=y[:, 2, cols(0)])
+        plane_quant(3)
+        plane_copy(0, [("S", 256), ("V", 256)])
+        plane_quant(0)
         for q in range(4):
             nc.sync.dma_start(
                 out=out_2[0, 4 * q : 4 * q + 4, :].bitcast(I32), in_=oqs[32 * q : 32 * q + 4, :].bitcast(I32)

@@ -21,9 +21,9 @@ T = 4
 C = 512
 NC = 4
 
-DOWN = "SSNN"
-YENG = "SSSV"
-EVAC = "0000"
+PIECES = [(0, 512), (512, 512), (1024, 512), (1536, 256), (1792, 256)]
+DOWN = "GGGG"
+YENG = "SSSS"
 
 
 def tile_gatedmemoryattentionlmhead_kernel(
@@ -37,10 +37,10 @@ def tile_gatedmemoryattentionlmhead_kernel(
         trp = ctx.enter_context(tc.psum_pool(name="trp", bufs=2))
         ctx.enter_context(tc.manual_schedule())
 
-        h_sb = keep.tile([P, 2, 2, D], BF16, name="h_sb")
-        h_gr = keep.tile([P, 2, 2, 2 * P, 4], BF16, name="h_gr", align_bytes=64)
-        hq = keep.tile([P, 2, 2, 2 * P], U32, name="hq", align_bytes=64)
-        hqs = keep.tile([P, 2, 2, 2 * P], U8, name="hqs", align_bytes=64)
+        h_sb = keep.tile([P, T, D], BF16, name="h_sb")
+        h_gr = keep.tile([P, T, 2, P, 4], BF16, name="h_gr", align_bytes=64)
+        hq = keep.tile([P, T, 2, P], U32, name="hq", align_bytes=64)
+        hqs = keep.tile([P, T, 2, P], U8, name="hqs", align_bytes=64)
         k_w = [keep.tile([P, 2, C], U32, name="k_w%d" % c, align_bytes=64) for c in range(NC)]
         w_w = [keep.tile([P, 2, C], U32, name="w_w%d" % c, align_bytes=64) for c in range(NC)]
         v_w = [keep.tile([P, 4, C], U32, name="v_w%d" % c, align_bytes=64) for c in range(NC)]
@@ -64,17 +64,22 @@ def tile_gatedmemoryattentionlmhead_kernel(
         nm = keep.tile([P, T], F32, name="nm")
         ssum = keep.tile([P, T], F32, name="ssum")
         rs = keep.tile([P, T], F32, name="rs")
-        lns = keep.tile([P, T], F32, name="lns")
-        ell = keep.tile([P, T], F32, name="ell")
-        lsum = keep.tile([P, 1], F32, name="lsum")
-        b4 = keep.tile([P, 1], F32, name="b4")
-        ed = keep.tile([P, T], F32, name="ed")
+        mbar = keep.tile([P, 1], F32, name="mbar")
+        em = keep.tile([P, T], F32, name="em")
+        expo = keep.tile([P, T], F32, name="expo")
+        root = keep.tile([P, T], F32, name="root")
+        rj = keep.tile([P, T], F32, name="rj")
+        rp = keep.tile([P, 1], F32, name="rp")
+        gj = keep.tile([P, P], F32, name="gj")
+        gm = keep.tile([P, 1], F32, name="gm")
+        u1 = keep.tile([P, T], F32, name="u1")
+        u2 = keep.tile([P, T], F32, name="u2")
+        u4 = keep.tile([P, T], F32, name="u4")
         den = keep.tile([P, T], F32, name="den")
         lam = keep.tile([P, T], F32, name="lam")
         c0 = keep.tile([P, T], F32, name="c0")
         c1 = keep.tile([P, T], F32, name="c1")
         zmx = keep.tile([P, T, NC], F32, name="zmx")
-        zj = keep.tile([P, NC], F32, name="zj")
         znm = keep.tile([P, T], F32, name="znm")
         zs4 = keep.tile([P, T, NC], F32, name="zs4")
         zs = keep.tile([P, T], F32, name="zs")
@@ -99,14 +104,15 @@ def tile_gatedmemoryattentionlmhead_kernel(
                 in_=src[:, :, cols(c), :].rearrange("q p n t -> p q (n t)").bitcast(I32),
             )
 
-        nc.sync.dma_start(out=h_sb[:, 0, :, :], in_=h_v[:, 0:2, :])
+        nc.sync.dma_start(out=h_sb[:, 0, :], in_=h_v[:, 0, :])
         nc.vector.memset(kb_row[:], 0.0)
         nc.vector.memset(k_sc[:].bitcast(I32), 0)
         nc.vector.memset(w_sc[:].bitcast(I32), 0)
         nc.vector.memset(v_sc[:].bitcast(I32), 0)
         nc.vector.memset(ones[:], 1.0)
         nc.vector.memset(eights[:], 8.0)
-        nc.vector.memset(mean_w[:], 4.0 / N)
+        nc.vector.memset(mean_w[:], -1.0 / N)
+        nc.vector.memset(expo[:], 1.0 / N)
         nc.vector.memset(warm[:], 0.0)
         make_identity(nc, ident[:])
         nc.gpsimd.memset(g_row[:], 0.0)
@@ -114,9 +120,10 @@ def tile_gatedmemoryattentionlmhead_kernel(
         nc.sync.dma_start(out=kb_row[0:1, :], in_=kb.rearrange("(o n) -> o n", o=1))
         load_scales(k_sc, keys_scales, 2)
         load_words(k_w, keys_words, 0)
+        nc.sync.dma_start(out=h_sb[:, 1, :], in_=h_v[:, 1, :])
         for c in range(1, NC):
             load_words(k_w, keys_words, c)
-        nc.sync.dma_start(out=h_sb[:, 1, :, :], in_=h_v[:, 2:4, :])
+        nc.sync.dma_start(out=h_sb[:, 2:4, :], in_=h_v[:, 2:4, :])
         nc.sync.dma_start(out=g_row[0:1, :], in_=g.rearrange("(o n) -> o n", o=1))
         load_scales(w_sc, w_lm_scales, 2)
         for c in range(NC):
@@ -126,32 +133,29 @@ def tile_gatedmemoryattentionlmhead_kernel(
             load_words(v_w, val_words, c)
 
         h_words = h_gr[:].rearrange("p s q n j -> p (s q n j)").bitcast(F32)
-
         h_ps = {}
 
-        def hturn(s2):
+        def hturn(t):
+            ps = trp.tile([P, 2, 2, P], F32, name="tr")
+            h_ps[t] = ps
             for q in range(2):
-                ps = trp.tile([P, 2, 2, P], F32, name="tr")
-                h_ps[(s2, q)] = ps
-                for i in range(2):
-                    wv = h_sb[:, s2, i, cols(q)].bitcast(F32)
-                    for u in range(2):
-                        nc.tensor.transpose(ps[:, i, u, :], wv[:, u : C // 2 : 2], ident[:])
+                wv = h_sb[:, t, cols(q)].bitcast(F32)
+                for u in range(2):
+                    nc.tensor.transpose(ps[:, q, u, :], wv[:, u : C // 2 : 2], ident[:])
 
-        def hcopy(s2, q):
-            lo = s2 * 1024 + q * 512
-            dst = h_words[:, lo : lo + 512].rearrange("p (i r u) -> p i r u", i=2, u=2)
-            src = h_ps[(s2, q)][:].rearrange("p i u r -> p i r u")
-            if q == 0:
+        def hcopy(t, eng):
+            dst = h_words[:, t * 512 : t * 512 + 512].rearrange("p (q r u) -> p q r u", q=2, u=2)
+            src = h_ps[t][:].rearrange("p q u r -> p q r u")
+            if eng == "V":
                 nc.vector.tensor_copy(out=dst, in_=src)
             else:
                 nc.scalar.copy(out=dst, in_=src)
 
-        def hquant(s2):
+        def hquant(t, n):
             nc.vector.quantize_mx(
-                out=hq[:, s2, :, :].rearrange("p q n -> p (q n)").bitcast(FP8X4),
-                scales=hqs[:, s2, :, :].rearrange("p q n -> p (q n)"),
-                in_=h_gr[:, s2, :, :, :].rearrange("p q n j -> p (q n j)"),
+                out=hq[:, t : t + n, :, :].rearrange("p s q n -> p (s q n)").bitcast(FP8X4),
+                scales=hqs[:, t : t + n, :, :].rearrange("p s q n -> p (s q n)"),
+                in_=h_gr[:, t : t + n, :, :, :].rearrange("p s q n j -> p (s q n j)"),
             )
 
         sp_ps = {}
@@ -179,21 +183,21 @@ def tile_gatedmemoryattentionlmhead_kernel(
         kc_t = {}
         ob_t = {}
 
-        def mx(ps, stat, stat_s, words, sc, c, n):
+        def mx(ps, stat, stat_s, words, sc, lo, w, n):
+            c, o = lo // C, lo % C
             for q in range(n):
                 nc.tensor.matmul_mx(
                     out=ps[:],
                     lhsT=stat[q],
                     lhsT_scale=stat_s[q],
-                    rhs=words[c][:, q, :].bitcast(FP8X4),
-                    rhs_scale=sc[4 * q : P, cols(c)],
+                    rhs=words[c][:, q, o : o + w].bitcast(FP8X4),
+                    rhs_scale=sc[4 * q : P, lo : lo + w],
                     start=(q == 0),
                     stop=(q == n - 1),
                 )
 
         def hstat(t):
-            sl = slice((t % 2) * P, (t % 2 + 1) * P)
-            return [hq[:, t // 2, q, sl].bitcast(FP8X4) for q in range(2)], [hqs[:, t // 2, q, sl] for q in range(2)]
+            return [hq[:, t, q, :].bitcast(FP8X4) for q in range(2)], [hqs[:, t, q, :] for q in range(2)]
 
         def score(t, c):
             st, ss = hstat(t)
@@ -202,7 +206,7 @@ def tile_gatedmemoryattentionlmhead_kernel(
                 if DOWN[t] != "N":
                     sb_t[t] = work.tile([P, M], BF16, name="sb", bufs=2)
             ps = acc.tile([P, C], F32, name="ps")
-            mx(ps, st, ss, k_w, k_sc, c, 2)
+            mx(ps, st, ss, k_w, k_sc, c * C, C, 2)
             nc.vector.scalar_tensor_tensor(
                 out=s_t[t][:, cols(c)], in0=ps[:], scalar=1.0 / 20.0, in1=kb_b[:, cols(c)], op0=OP.mult, op1=OP.add
             )
@@ -269,17 +273,15 @@ def tile_gatedmemoryattentionlmhead_kernel(
             z_ps[t] = []
             for c in range(NC):
                 ps = acc.tile([P, C], F32, name="ps")
-                mx(ps, st, ss, w_w, w_sc, c, 2)
+                mx(ps, st, ss, w_w, w_sc, c * C, C, 2)
                 z_ps[t].append(ps)
 
         def zmax(t, half):
             for c in (2 * half, 2 * half + 1):
-                nc.vector.tensor_reduce(out=zmx[:, t, c : c + 1], in_=z_ps[t][c][:], axis=AX.X, op=OP.max)
+                nc.vector.tensor_reduce(out=zmx[:, t, c : c + 1], in_=z_ps[t][c][:], axis=AX.X, op=OP.max, negate=True)
 
         def zneg(t):
-            nc.vector.tensor_scalar(
-                out=zj[:], in0=zmx[:, t, :], scalar1=-1.0, scalar2=None, op0=OP.mult, op1=OP.min, accum_out=znm[:, t : t + 1]
-            )
+            nc.vector.tensor_reduce(out=znm[:, t : t + 1], in_=zmx[:, t, :], axis=AX.X, op=OP.min)
 
         def zexp(t):
             for c in range(NC):
@@ -299,31 +301,52 @@ def tile_gatedmemoryattentionlmhead_kernel(
                 out=c1[:, t : t + 1], in0=rz[:, t : t + 1], scalar1=c0[:, t : t + 1], scalar2=-float(V), op0=OP.mult, op1=OP.mult
             )
 
-        gate_ps = []
+        gate_ps = {}
+
+        def gn1():
+            ps = acc.tile([P, T], F32, name="ps")
+            nc.tensor.matmul(ps[:], lhsT=mean_w[:], rhs=nm[:], start=True, stop=True)
+            gate_ps["m"] = ps
+
+        def gn2():
+            nc.vector.tensor_reduce(out=mbar[:], in_=gate_ps["m"][:], axis=AX.X, op=OP.add)
+
+        def gn3():
+            nc.scalar.activation(out=em[:], in_=nm[:], func=ACT.Exp, bias=mbar[:])
 
         def g1():
-            nc.scalar.activation(out=lns[:], in_=ssum[:], func=ACT.Ln)
+            nc.gpsimd.tensor_tensor(out=root[:], in0=ssum[:], in1=expo[:], op=OP.pow)
 
         def g2():
-            nc.vector.scalar_tensor_tensor(
-                out=ell[:], in0=lns[:], scalar=1.0, in1=nm[:], op0=OP.mult, op1=OP.subtract, accum_out=lsum[:]
+            nc.vector.tensor_scalar(
+                out=rj[:], in0=root[:], scalar1=1.0, scalar2=None, op0=OP.mult, op1=OP.mult, accum_out=rp[:]
             )
 
         def g3():
-            ps = acc.tile([P, C], F32, name="ps")
-            nc.tensor.matmul(ps[:, 0:1], lhsT=mean_w[:], rhs=lsum[:], start=True, stop=True)
-            gate_ps.append(ps)
+            ps = acc.tile([P, P], F32, name="ps")
+            nc.tensor.matmul(ps[:], lhsT=rp[:].to_broadcast([P, P]), rhs=ident[:], start=True, stop=True)
+            gate_ps["r"] = ps
 
         def g4():
-            nc.vector.tensor_copy(out=b4[:], in_=gate_ps[0][:, 0:1])
+            nc.vector.tensor_scalar(
+                out=gj[:], in0=gate_ps["r"][:], scalar1=1.0, scalar2=None, op0=OP.mult, op1=OP.mult, accum_out=gm[:]
+            )
 
         def g5():
-            nc.scalar.activation(out=ed[:], in_=ell[:], func=ACT.Exp, bias=b4[:], scale=-4.0)
+            nc.vector.scalar_tensor_tensor(
+                out=u1[:], in0=rs[:], scalar=gm[:], in1=em[:], op0=OP.mult, op1=OP.mult
+            )
 
         def g6():
-            nc.vector.tensor_scalar(out=den[:], in0=ed[:], scalar1=1.0, scalar2=None, op0=OP.add)
+            nc.vector.tensor_tensor(out=u2[:], in0=u1[:], in1=u1[:], op=OP.mult)
 
         def g6b():
+            nc.vector.tensor_tensor(out=u4[:], in0=u2[:], in1=u2[:], op=OP.mult)
+
+        def g6c():
+            nc.vector.tensor_scalar(out=den[:], in0=u4[:], scalar1=1.0, scalar2=None, op0=OP.add)
+
+        def g6d():
             nc.vector.reciprocal(out=lam[:], in_=den[:])
 
         def g7():
@@ -342,216 +365,216 @@ def tile_gatedmemoryattentionlmhead_kernel(
                 )
 
         def kmm(t, c):
-            ps = acc.tile([P, C], F32, name="ps")
+            lo, w = PIECES[c]
+            ps = acc.tile([P, w], F32, name="ps")
             st = [aq[t][:, q, :].bitcast(FP8X4) for q in range(4)]
             ss = [aqs[t][:, q, :] for q in range(4)]
-            mx(ps, st, ss, v_w, v_sc, c, 4)
+            mx(ps, st, ss, v_w, v_sc, lo, w, 4)
             k_ps[(t, c)] = ps
-
-        def evac(t, c):
-            if t not in kc_t:
-                kc_t[t] = work.tile([P, V], F32, name="s", bufs=4)
-            nc.scalar.copy(out=kc_t[t][:, cols(c)], in_=k_ps[(t, c)][:])
 
         o_v = out_0.rearrange("(p t) m -> p t m", t=T)
 
         def mix(t, c):
+            lo, w = PIECES[c]
+            sl = slice(lo, lo + w)
             nc.vector.scalar_tensor_tensor(
-                out=y[:, t, cols(c)], in0=kc_t[t][:, cols(c)] if EVAC[t] == "1" else k_ps[(t, c)][:], scalar=lam[:, t : t + 1], in1=y[:, t, cols(c)], op0=OP.mult, op1=OP.add
+                out=y[:, t, sl], in0=k_ps[(t, c)][:], scalar=lam[:, t : t + 1], in1=y[:, t, sl], op0=OP.mult, op1=OP.add
             )
+            nc.sync.dma_start(out=o_v[:, t, sl], in_=y[:, t, sl])
 
         def plane_copy(c, shares):
+            lo, w = PIECES[c]
             ob_t[c] = work.tile([P, C, 4], BF16, name="ob", bufs=2, align_bytes=64)
-            lo = 0
+            o = 0
             for eng, n in shares:
-                dst = ob_t[c][:, lo : lo + n, :]
-                src = y[:, :, c * C + lo : c * C + lo + n].rearrange("p t m -> p m t")
+                dst = ob_t[c][:, o : o + n, :]
+                src = y[:, :, lo + o : lo + o + n].rearrange("p t m -> p m t")
                 if eng == "S":
                     nc.scalar.copy(out=dst, in_=src)
                 else:
                     nc.vector.tensor_copy(out=dst, in_=src)
-                lo += n
+                o += n
 
         def plane_quant(c):
+            lo, w = PIECES[c]
+            sl = slice(lo, lo + w)
             nc.vector.quantize_mx(
-                out=oq[:, cols(c)].bitcast(FP8X4), scales=oqs[:, cols(c)], in_=ob_t[c][:].rearrange("p m j -> p (m j)")
+                out=oq[:, sl].bitcast(FP8X4), scales=oqs[:, sl], in_=ob_t[c][:, 0:w, :].rearrange("p m j -> p (m j)")
             )
             nc.sync.dma_start(
-                out=out_1[0, :, cols(c), :].rearrange("p n t -> p (n t)").bitcast(I32), in_=oq[:, cols(c)].bitcast(I32)
+                out=out_1[0, :, sl, :].rearrange("p n t -> p (n t)").bitcast(I32), in_=oq[:, sl].bitcast(I32)
             )
 
         hturn(0)
-        hcopy(0, 0)
-        hcopy(0, 1)
+        hcopy(0, "V")
         spread_mm("kb", ones, kb_row)
         spread_copy("kb", kb_b)
-        hquant(0)
+        hquant(0, 1)
         score(0, 0)
-        score(1, 0)
-        score(1, 1)
+        hturn(1)
+        hcopy(1, "S")
+        hquant(1, 1)
         score(0, 1)
+        score(1, 0)
         score(0, 2)
-        down(1, 0)
-        down(0, 0)
-        score(1, 2)
+        score(1, 1)
         score(0, 3)
         score(1, 3)
-        hturn(1)
-        down(0, 1)
-        hcopy(1, 0)
-        hcopy(1, 1)
-        down(1, 1)
+        score(1, 2)
+        hturn(2)
+        hturn(3)
+        hcopy(2, "S")
         smax(0)
-        spread_mm("g", eights, g_row)
-        hquant(1)
+        hcopy(3, "S")
+        hquant(2, 2)
         smax(1)
-        score(3, 1)
-        score(3, 0)
-        spread_copy("g", g_b)
-        score(2, 3)
-        score(2, 1)
-        score(3, 3)
-        score(3, 2)
-        zmm(0)
-        zmax(0, 0)
-        zmax(0, 1)
-        score(2, 0)
         sexp(0)
-        zneg(0)
+        spread_mm("g", eights, g_row)
+        spread_copy("g", g_b)
+        score(3, 3)
+        score(2, 1)
         score(2, 2)
-        smax(3)
         sexp(1)
-        zexp(0)
-        zmm(1)
-        sexp(3)
-        smax(2)
         srec(0)
-        zsum(0)
-        gain(0, 0)
+        score(3, 0)
+        score(3, 2)
+        score(3, 1)
+        zmm(1)
         zmax(1, 0)
-        sexp(2)
         zmax(1, 1)
-        zinv(0)
-        turn(0, 0)
-        tcopy(0, 0)
-        srec(1)
+        score(2, 3)
         zneg(1)
-        g1()
-        gain(0, 1)
-        turn(0, 1)
-        g2()
+        score(2, 0)
+        smax(3)
         zexp(1)
-        g3()
-        zmm(2)
+        smax(2)
+        srec(1)
+        zmm(0)
+        zmax(0, 1)
+        zmax(0, 0)
+        gain(0, 0)
+        sexp(3)
+        turn(0, 0)
+        gn1()
+        zneg(0)
+        sexp(2)
+        gain(0, 1)
+        zexp(0)
         gain(1, 0)
-        gain(1, 1)
+        zmm(2)
+        turn(0, 1)
         zmax(2, 0)
-        g4()
         zmax(2, 1)
-        tcopy(0, 1)
-        g5()
-        turn(1, 0)
-        g6()
+        g1()
+        g2()
         zneg(2)
-        zexp(2)
-        turn(1, 1)
+        tcopy(0, 0)
+        tcopy(0, 1)
+        turn(1, 0)
+        srec(2)
+        gn2()
         aquant(0)
-        zmm(3)
-        g6b()
-        srec(3)
-        kmm(0, 2)
-        zmax(3, 0)
-        g7()
-        zmax(3, 1)
-        tcopy(1, 1)
+        zexp(2)
+        gain(1, 1)
+        g3()
         tcopy(1, 0)
+        zmm(3)
+        turn(1, 1)
+        gn3()
+        zmax(3, 0)
+        kmm(0, 0)
+        zmax(3, 1)
+        srec(3)
+        g4()
+        kmm(0, 2)
+        zneg(3)
+        zsum(0)
+        g5()
         zsum(1)
         zsum(2)
-        kmm(0, 1)
-        zneg(3)
-        zinv(1)
-        gain(3, 1)
+        tcopy(1, 1)
+        g6()
         aquant(1)
         zexp(3)
-        kmm(0, 0)
-        srec(2)
-        zc1(0)
-        kmm(1, 2)
-        yaff(0)
-        gain(3, 0)
-        zsum(3)
-        gain(2, 0)
-        zc1(1)
-        turn(3, 1)
-        gain(2, 1)
-        tcopy(3, 1)
-        turn(3, 0)
-        mix(0, 1)
-        nc.sync.dma_start(out=o_v[:, 0, cols(1)], in_=y[:, 0, cols(1)])
+        g6b()
+        kmm(0, 4)
+        zinv(1)
         zinv(2)
-        kmm(0, 3)
-        turn(2, 0)
-        mix(0, 0)
-        nc.sync.dma_start(out=o_v[:, 0, cols(0)], in_=y[:, 0, cols(0)])
-        tcopy(3, 0)
+        g6c()
+        zinv(0)
+        g6d()
+        kmm(0, 1)
+        g7()
+        zc1(0)
+        yaff(0)
+        zc1(1)
+        gain(2, 1)
+        gain(2, 0)
+        kmm(1, 2)
         turn(2, 1)
-        zc1(2)
-        mix(0, 2)
-        nc.sync.dma_start(out=o_v[:, 0, cols(2)], in_=y[:, 0, cols(2)])
-        tcopy(2, 0)
+        zsum(3)
         tcopy(2, 1)
-        zinv(3)
-        yaff(1)
-        aquant(3)
-        zc1(3)
-        kmm(1, 3)
-        aquant(2)
-        yaff(3)
-        kmm(1, 1)
-        mix(1, 1)
-        nc.sync.dma_start(out=o_v[:, 1, cols(1)], in_=y[:, 1, cols(1)])
-        kmm(3, 1)
-        yaff(2)
-        mix(1, 2)
-        nc.sync.dma_start(out=o_v[:, 1, cols(2)], in_=y[:, 1, cols(2)])
-        kmm(2, 1)
-        kmm(3, 2)
-        mix(3, 1)
-        nc.sync.dma_start(out=o_v[:, 3, cols(1)], in_=y[:, 3, cols(1)])
-        mix(0, 3)
-        nc.sync.dma_start(out=o_v[:, 0, cols(3)], in_=y[:, 0, cols(3)])
-        mix(1, 3)
-        nc.sync.dma_start(out=o_v[:, 1, cols(3)], in_=y[:, 1, cols(3)])
-        kmm(2, 2)
-        mix(2, 1)
-        nc.sync.dma_start(out=o_v[:, 2, cols(1)], in_=y[:, 2, cols(1)])
-        kmm(3, 3)
-        kmm(2, 3)
-        mix(3, 2)
-        nc.sync.dma_start(out=o_v[:, 3, cols(2)], in_=y[:, 3, cols(2)])
-        plane_copy(1, [("S", 256), ("V", 256)])
-        kmm(3, 0)
-        mix(2, 2)
-        nc.sync.dma_start(out=o_v[:, 2, cols(2)], in_=y[:, 2, cols(2)])
-        plane_quant(1)
+        mix(0, 0)
+        gain(3, 1)
+        turn(2, 0)
+        kmm(1, 4)
+        gain(3, 0)
+        tcopy(2, 0)
+        mix(0, 2)
+        mix(0, 4)
         kmm(1, 0)
-        plane_copy(2, [("S", 256), ("V", 256)])
-        mix(3, 3)
-        nc.sync.dma_start(out=o_v[:, 3, cols(3)], in_=y[:, 3, cols(3)])
-        mix(2, 3)
-        nc.sync.dma_start(out=o_v[:, 2, cols(3)], in_=y[:, 2, cols(3)])
+        turn(3, 1)
+        aquant(2)
+        turn(3, 0)
+        zc1(2)
+        kmm(0, 3)
+        yaff(1)
+        mix(1, 4)
+        zinv(3)
+        mix(0, 1)
+        mix(1, 2)
+        tcopy(3, 1)
+        tcopy(3, 0)
+        kmm(2, 2)
+        zc1(3)
         kmm(2, 0)
-        plane_quant(2)
-        mix(3, 0)
-        nc.sync.dma_start(out=o_v[:, 3, cols(0)], in_=y[:, 3, cols(0)])
-        plane_copy(3, [("S", 256), ("V", 256)])
+        aquant(3)
         mix(1, 0)
-        nc.sync.dma_start(out=o_v[:, 1, cols(0)], in_=y[:, 1, cols(0)])
+        yaff(2)
+        yaff(3)
         mix(2, 0)
-        nc.sync.dma_start(out=o_v[:, 2, cols(0)], in_=y[:, 2, cols(0)])
-        plane_quant(3)
-        plane_copy(0, [("S", 256), ("V", 256)])
+        kmm(2, 4)
+        mix(0, 3)
+        kmm(3, 2)
+        kmm(3, 4)
+        mix(2, 2)
+        mix(2, 4)
+        mix(3, 2)
+        mix(3, 4)
+        kmm(3, 0)
+        plane_copy(4, [("S", 88), ("V", 168)])
+        kmm(3, 1)
+        mix(3, 0)
+        plane_copy(2, [("S", 408), ("V", 104)])
+        plane_quant(4)
+        mix(3, 1)
+        plane_copy(0, [("S", 408), ("V", 104)])
+        plane_quant(2)
+        kmm(2, 1)
+        kmm(1, 1)
+        kmm(2, 3)
+        mix(2, 1)
+        mix(1, 1)
+        mix(2, 3)
+        kmm(1, 3)
+        kmm(3, 3)
         plane_quant(0)
+        mix(1, 3)
+        mix(3, 3)
+        plane_copy(1, [("S", 408), ("V", 104)])
+        plane_copy(3, [("S", 88), ("V", 168)])
+        plane_quant(1)
+        plane_quant(3)
         for q in range(4):
             nc.sync.dma_start(
                 out=out_2[0, 4 * q : 4 * q + 4, :].bitcast(I32), in_=oqs[32 * q : 32 * q + 4, :].bitcast(I32)

from contextlib import ExitStack

import concourse.mybir as mybir
from concourse.masks import make_identity

N, D, M, V = 512, 1024, 2048, 2048
FLOPS = 2 * N * (D * M + D * V + M * V)

F32 = mybir.dt.float32
BF16 = mybir.dt.bfloat16
U32 = mybir.dt.uint32
I32 = mybir.dt.int32
U8 = mybir.dt.uint8
FP8X4 = mybir.dt.float8_e4m3fn_x4
ACT = mybir.ActivationFunctionType
OP = mybir.AluOpType
AX = mybir.AxisListType

P = 128
T = 4
C = 512
NC = 4

PIECES = [(0, 512), (512, 512), (1024, 512), (1536, 256), (1792, 256)]
DOWN = "GGGG"
YENG = "SSSS"


def tile_gatedmemoryattentionlmhead_kernel(
    tc, h, keys_words, keys_scales, kb, g, val_words, val_scales, w_lm_words, w_lm_scales, out_0, out_1, out_2
):
    nc = tc.nc
    with ExitStack() as ctx:
        keep = ctx.enter_context(tc.tile_pool(name="keep", bufs=1))
        work = ctx.enter_context(tc.tile_pool(name="work", bufs=2))
        acc = ctx.enter_context(tc.psum_pool(name="acc", bufs=6))
        trp = ctx.enter_context(tc.psum_pool(name="trp", bufs=2))
        ctx.enter_context(tc.manual_schedule())

        h_sb = keep.tile([P, T, D], BF16, name="h_sb")
        h_gr = keep.tile([P, T, 2, P, 4], BF16, name="h_gr", align_bytes=64)
        hq = keep.tile([P, T, 2, P], U32, name="hq", align_bytes=64)
        hqs = keep.tile([P, T, 2, P], U8, name="hqs", align_bytes=64)
        k_w = [keep.tile([P, 2, C], U32, name="k_w%d" % c, align_bytes=64) for c in range(NC)]
        w_w = [keep.tile([P, 2, C], U32, name="w_w%d" % c, align_bytes=64) for c in range(NC)]
        v_w = [keep.tile([P, 4, C], U32, name="v_w%d" % c, align_bytes=64) for c in range(NC)]
        k_sc = keep.tile([P, M], U8, name="k_sc", align_bytes=64)
        w_sc = keep.tile([P, V], U8, name="w_sc", align_bytes=64)
        v_sc = keep.tile([P, V], U8, name="v_sc", align_bytes=64)
        kb_row = keep.tile([P, M], BF16, name="kb_row")
        g_row = keep.tile([P, M], BF16, name="g_row")
        kb_b = keep.tile([P, M], BF16, name="kb_b")
        g_b = keep.tile([P, M], BF16, name="g_b")
        ones = keep.tile([P, P], BF16, name="ones")
        eights = keep.tile([P, P], BF16, name="eights")
        mean_w = keep.tile([P, P], F32, name="mean_w")
        ident = keep.tile([P, P], F32, name="ident")
        aq = [keep.tile([P, 4, P], U32, name="aq%d" % t, align_bytes=64) for t in range(T)]
        aqs = [keep.tile([P, 4, P], U8, name="aqs%d" % t, align_bytes=64) for t in range(T)]
        y = keep.tile([P, T, V], F32, name="y")
        oq = keep.tile([P, V], U32, name="oq", align_bytes=64)
        oqs = keep.tile([P, V], U8, name="oqs", align_bytes=64)
        junk = keep.tile([P, M], BF16, name="junk")
        nm = keep.tile([P, T], F32, name="nm")
        ssum = keep.tile([P, T], F32, name="ssum")
        rs = keep.tile([P, T], F32, name="rs")
        mbar = keep.tile([P, 1], F32, name="mbar")
        em = keep.tile([P, T], F32, name="em")
        expo = keep.tile([P, T], F32, name="expo")
        root = keep.tile([P, T], F32, name="root")
        rj = keep.tile([P, T], F32, name="rj")
        rp = keep.tile([P, 1], F32, name="rp")
        gj = keep.tile([P, P], F32, name="gj")
        gm = keep.tile([P, 1], F32, name="gm")
        u1 = keep.tile([P, T], F32, name="u1")
        u2 = keep.tile([P, T], F32, name="u2")
        u4 = keep.tile([P, T], F32, name="u4")
        den = keep.tile([P, T], F32, name="den")
        lam = keep.tile([P, T], F32, name="lam")
        c0 = keep.tile([P, T], F32, name="c0")
        c1 = keep.tile([P, T], F32, name="c1")
        zmx = keep.tile([P, T, NC], F32, name="zmx")
        znm = keep.tile([P, T], F32, name="znm")
        zs4 = keep.tile([P, T, NC], F32, name="zs4")
        zs = keep.tile([P, T], F32, name="zs")
        rz = keep.tile([P, T], F32, name="rz")
        warm = keep.tile([P, 1], F32, name="warm")

        def cols(c):
            return slice(c * C, (c + 1) * C)

        h_v = h.rearrange("(p t) k -> p t k", t=T)

        def load_scales(tile, src, n):
            for q in range(4):
                nc.sync.dma_start(
                    out=tile[32 * q : 32 * q + 4 * n, :].bitcast(I32),
                    in_=src[:, 4 * q : 4 * q + 4, :].bitcast(I32),
                )

        def load_words(tiles, src, c):
            nc.sync.dma_start(
                out=tiles[c][:].bitcast(I32),
                in_=src[:, :, cols(c), :].rearrange("q p n t -> p q (n t)").bitcast(I32),
            )

        nc.sync.dma_start(out=h_sb[:, 0, :], in_=h_v[:, 0, :])
        nc.vector.memset(kb_row[:], 0.0)
        nc.vector.memset(k_sc[:].bitcast(I32), 0)
        nc.vector.memset(w_sc[:].bitcast(I32), 0)
        nc.vector.memset(v_sc[:].bitcast(I32), 0)
        nc.vector.memset(ones[:], 1.0)
        nc.vector.memset(eights[:], 8.0)
        nc.vector.memset(mean_w[:], -1.0 / N)
        nc.vector.memset(expo[:], 1.0 / N)
        nc.vector.memset(warm[:], 0.0)
        make_identity(nc, ident[:])
        nc.gpsimd.memset(g_row[:], 0.0)
        nc.scalar.activation(out=warm[:], in_=warm[:], func=ACT.Exp)
        nc.sync.dma_start(out=kb_row[0:1, :], in_=kb.rearrange("(o n) -> o n", o=1))
        load_scales(k_sc, keys_scales, 2)
        load_words(k_w, keys_words, 0)
        nc.sync.dma_start(out=h_sb[:, 1, :], in_=h_v[:, 1, :])
        for c in range(1, NC):
            load_words(k_w, keys_words, c)
        nc.sync.dma_start(out=h_sb[:, 2:4, :], in_=h_v[:, 2:4, :])
        nc.sync.dma_start(out=g_row[0:1, :], in_=g.rearrange("(o n) -> o n", o=1))
        load_scales(w_sc, w_lm_scales, 2)
        for c in range(NC):
            load_words(w_w, w_lm_words, c)
        load_scales(v_sc, val_scales, 4)
        for c in range(NC):
            load_words(v_w, val_words, c)

        h_words = h_gr[:].rearrange("p s q n j -> p (s q n j)").bitcast(F32)
        h_ps = {}

        def hturn(t):
            ps = trp.tile([P, 2, 2, P], F32, name="tr")
            h_ps[t] = ps
            for q in range(2):
                wv = h_sb[:, t, cols(q)].bitcast(F32)
                for u in range(2):
                    nc.tensor.transpose(ps[:, q, u, :], wv[:, u : C // 2 : 2], ident[:])

        def hcopy(t, eng):
            dst = h_words[:, t * 512 : t * 512 + 512].rearrange("p (q r u) -> p q r u", q=2, u=2)
            src = h_ps[t][:].rearrange("p q u r -> p q r u")
            if eng == "V":
                nc.vector.tensor_copy(out=dst, in_=src)
            else:
                nc.scalar.copy(out=dst, in_=src)

        def hquant(t, n):
            nc.vector.quantize_mx(
                out=hq[:, t : t + n, :, :].rearrange("p s q n -> p (s q n)").bitcast(FP8X4),
                scales=hqs[:, t : t + n, :, :].rearrange("p s q n -> p (s q n)"),
                in_=h_gr[:, t : t + n, :, :, :].rearrange("p s q n j -> p (s q n j)"),
            )

        sp_ps = {}

        def spread_mm(key, lhs, row):
            for half in range(2):
                ps = acc.tile([P, 1024], BF16, name="ps")
                sp_ps[(key, half)] = ps
                for i in range(2):
                    lo = half * 1024 + i * C
                    nc.tensor.matmul(
                        ps[:, i * C : (i + 1) * C], lhsT=lhs[:], rhs=row[:, lo : lo + C], start=True, stop=True
                    )

        def spread_copy(key, dst):
            for half in range(2):
                nc.scalar.copy(out=dst[:, half * 1024 : half * 1024 + 1024], in_=sp_ps[(key, half)][:])

        s_t = {}
        sb_t = {}
        a_t = {}
        ga_t = {}
        z_ps = {}
        k_ps = {}
        kc_t = {}
        ob_t = {}

        def mx(ps, stat, stat_s, words, sc, lo, w, n):
            c, o = lo // C, lo % C
            for q in range(n):
                nc.tensor.matmul_mx(
                    out=ps[:],
                    lhsT=stat[q],
                    lhsT_scale=stat_s[q],
                    rhs=words[c][:, q, o : o + w].bitcast(FP8X4),
                    rhs_scale=sc[4 * q : P, lo : lo + w],
                    start=(q == 0),
                    stop=(q == n - 1),
                )

        def hstat(t):
            return [hq[:, t, q, :].bitcast(FP8X4) for q in range(2)], [hqs[:, t, q, :] for q in range(2)]

        def score(t, c):
            st, ss = hstat(t)
            if t not in s_t:
                s_t[t] = work.tile([P, M], F32, name="s", bufs=4)
                if DOWN[t] != "N":
                    sb_t[t] = work.tile([P, M], BF16, name="sb", bufs=2)
            ps = acc.tile([P, C], F32, name="ps")
            mx(ps, st, ss, k_w, k_sc, c * C, C, 2)
            nc.vector.scalar_tensor_tensor(
                out=s_t[t][:, cols(c)], in0=ps[:], scalar=1.0 / 20.0, in1=kb_b[:, cols(c)], op0=OP.mult, op1=OP.add
            )
            if DOWN[t] == "G":
                nc.gpsimd.tensor_scalar(
                    out=sb_t[t][:, cols(c)], in0=s_t[t][:, cols(c)], scalar1=1.0, scalar2=0.0, op0=OP.mult, op1=OP.add
                )

        def down(t, half):
            sl = slice(half * 1024, half * 1024 + 1024)
            nc.scalar.copy(out=sb_t[t][:, sl], in_=s_t[t][:, sl])

        def smax(t):
            nc.vector.tensor_scalar(
                out=junk[:], in0=(s_t if DOWN[t] == "N" else sb_t)[t][:], scalar1=-1.0, scalar2=None, op0=OP.mult, op1=OP.min,
                accum_out=nm[:, t : t + 1],
            )

        def sexp(t):
            nc.scalar.activation(
                out=s_t[t][:], in_=s_t[t][:], func=ACT.Exp, bias=nm[:, t : t + 1], accum_out=ssum[:, t : t + 1]
            )

        def srec(t):
            nc.vector.reciprocal(out=rs[:, t : t + 1], in_=ssum[:, t : t + 1])

        def gain(t, half):
            if t not in a_t:
                a_t[t] = work.tile([P, M], BF16, name="a", bufs=2)
            sl = slice(half * 1024, half * 1024 + 1024)
            nc.vector.scalar_tensor_tensor(
                out=a_t[t][:, sl], in0=s_t[t][:, sl], scalar=rs[:, t : t + 1], in1=g_b[:, sl], op0=OP.mult, op1=OP.mult
            )

        tr_ps = {}

        def turn(t, half):
            av = a_t[t][:].bitcast(F32)
            ps = trp.tile([P, 2, 2, P], F32, name="tr")
            tr_ps[(t, half)] = ps
            for i in range(2):
                q = 2 * half + i
                for u in range(2):
                    nc.tensor.transpose(ps[:, i, u, :], av[:, 256 * q + u : 256 * (q + 1) : 2], ident[:])

        def tcopy(t, half):
            if t not in ga_t:
                ga_t[t] = work.tile([P, 4, P, 4], BF16, name="ga", bufs=2, align_bytes=64)
            dw = ga_t[t][:].rearrange("p q r j -> p (q r j)").bitcast(F32)
            nc.scalar.copy(
                out=dw[:, half * 512 : half * 512 + 512].rearrange("p (i r u) -> p i r u", i=2, u=2),
                in_=tr_ps[(t, half)][:].rearrange("p i u r -> p i r u"),
            )

        def aquant(t):
            nc.vector.quantize_mx(
                out=aq[t][:].rearrange("p q r -> p (q r)").bitcast(FP8X4),
                scales=aqs[t][:].rearrange("p q r -> p (q r)"),
                in_=ga_t[t][:].rearrange("p q r j -> p (q r j)"),
            )

        def zmm(t):
            st, ss = hstat(t)
            z_ps[t] = []
            for c in range(NC):
                ps = acc.tile([P, C], F32, name="ps")
                mx(ps, st, ss, w_w, w_sc, c * C, C, 2)
                z_ps[t].append(ps)

        def zmax(t, half):
            for c in (2 * half, 2 * half + 1):
                nc.vector.tensor_reduce(out=zmx[:, t, c : c + 1], in_=z_ps[t][c][:], axis=AX.X, op=OP.max, negate=True)

        def zneg(t):
            nc.vector.tensor_reduce(out=znm[:, t : t + 1], in_=zmx[:, t, :], axis=AX.X, op=OP.min)

        def zexp(t):
            for c in range(NC):
                nc.scalar.activation(
                    out=y[:, t, cols(c)], in_=z_ps[t][c][:], func=ACT.Exp, bias=znm[:, t : t + 1],
                    accum_out=zs4[:, t, c : c + 1],
                )

        def zsum(t):
            nc.vector.tensor_reduce(out=zs[:, t : t + 1], in_=zs4[:, t, :], axis=AX.X, op=OP.add)

        def zinv(t):
            nc.vector.reciprocal(out=rz[:, t : t + 1], in_=zs[:, t : t + 1])

        def zc1(t):
            nc.vector.tensor_scalar(
                out=c1[:, t : t + 1], in0=rz[:, t : t + 1], scalar1=c0[:, t : t + 1], scalar2=-float(V), op0=OP.mult, op1=OP.mult
            )

        gate_ps = {}

        def gn1():
            ps = acc.tile([P, T], F32, name="ps")
            nc.tensor.matmul(ps[:], lhsT=mean_w[:], rhs=nm[:], start=True, stop=True)
            gate_ps["m"] = ps

        def gn2():
            nc.vector.tensor_reduce(out=mbar[:], in_=gate_ps["m"][:], axis=AX.X, op=OP.add)

        def gn3():
            nc.scalar.activation(out=em[:], in_=nm[:], func=ACT.Exp, bias=mbar[:])

        def g1():
            nc.gpsimd.tensor_tensor(out=root[:], in0=ssum[:], in1=expo[:], op=OP.pow)

        def g2():
            nc.vector.tensor_scalar(
                out=rj[:], in0=root[:], scalar1=1.0, scalar2=None, op0=OP.mult, op1=OP.mult, accum_out=rp[:]
            )

        def g3():
            ps = acc.tile([P, P], F32, name="ps")
            nc.tensor.matmul(ps[:], lhsT=rp[:].to_broadcast([P, P]), rhs=ident[:], start=True, stop=True)
            gate_ps["r"] = ps

        def g4():
            nc.vector.tensor_scalar(
                out=gj[:], in0=gate_ps["r"][:], scalar1=1.0, scalar2=None, op0=OP.mult, op1=OP.mult, accum_out=gm[:]
            )

        def g5():
            nc.vector.scalar_tensor_tensor(
                out=u1[:], in0=rs[:], scalar=gm[:], in1=em[:], op0=OP.mult, op1=OP.mult
            )

        def g6():
            nc.vector.tensor_tensor(out=u2[:], in0=u1[:], in1=u1[:], op=OP.mult)

        def g6b():
            nc.vector.tensor_tensor(out=u4[:], in0=u2[:], in1=u2[:], op=OP.mult)

        def g6c():
            nc.vector.tensor_scalar(out=den[:], in0=u4[:], scalar1=1.0, scalar2=None, op0=OP.add)

        def g6d():
            nc.vector.reciprocal(out=lam[:], in_=den[:])

        def g7():
            nc.vector.tensor_scalar(out=c0[:], in0=lam[:], scalar1=-1.0, scalar2=None, op0=OP.add)

        def yaff(t):
            for c in range(NC):
                if YENG[t] == "S":
                    nc.scalar.activation(
                        out=y[:, t, cols(c)], in_=y[:, t, cols(c)], func=ACT.Identity, bias=c0[:, t : t + 1], scale=c1[:, t : t + 1]
                    )
                    continue
                (nc.vector if YENG[t] == "V" else nc.gpsimd).tensor_scalar(
                    out=y[:, t, cols(c)], in0=y[:, t, cols(c)], scalar1=c1[:, t : t + 1], scalar2=c0[:, t : t + 1],
                    op0=OP.mult, op1=OP.add,
                )

        def kmm(t, c):
            lo, w = PIECES[c]
            ps = acc.tile([P, w], F32, name="ps")
            st = [aq[t][:, q, :].bitcast(FP8X4) for q in range(4)]
            ss = [aqs[t][:, q, :] for q in range(4)]
            mx(ps, st, ss, v_w, v_sc, lo, w, 4)
            k_ps[(t, c)] = ps

        o_v = out_0.rearrange("(p t) m -> p t m", t=T)

        def mix(t, c):
            lo, w = PIECES[c]
            sl = slice(lo, lo + w)
            nc.vector.scalar_tensor_tensor(
                out=y[:, t, sl], in0=k_ps[(t, c)][:], scalar=lam[:, t : t + 1], in1=y[:, t, sl], op0=OP.mult, op1=OP.add
            )
            nc.sync.dma_start(out=o_v[:, t, sl], in_=y[:, t, sl])

        def plane_copy(c, shares):
            lo, w = PIECES[c]
            ob_t[c] = work.tile([P, C, 4], BF16, name="ob", bufs=2, align_bytes=64)
            o = 0
            for eng, n in shares:
                dst = ob_t[c][:, o : o + n, :]
                src = y[:, :, lo + o : lo + o + n].rearrange("p t m -> p m t")
                if eng == "S":
                    nc.scalar.copy(out=dst, in_=src)
                else:
                    nc.vector.tensor_copy(out=dst, in_=src)
                o += n

        def plane_quant(c):
            lo, w = PIECES[c]
            sl = slice(lo, lo + w)
            nc.vector.quantize_mx(
                out=oq[:, sl].bitcast(FP8X4), scales=oqs[:, sl], in_=ob_t[c][:, 0:w, :].rearrange("p m j -> p (m j)")
            )
            nc.sync.dma_start(
                out=out_1[0, :, sl, :].rearrange("p n t -> p (n t)").bitcast(I32), in_=oq[:, sl].bitcast(I32)
            )

        hturn(0)
        hcopy(0, "V")
        spread_mm("kb", ones, kb_row)
        spread_copy("kb", kb_b)
        hquant(0, 1)
        score(0, 0)
        hturn(1)
        hcopy(1, "S")
        hquant(1, 1)
        score(0, 1)
        score(1, 0)
        score(0, 2)
        score(1, 1)
        score(0, 3)
        score(1, 3)
        score(1, 2)
        hturn(2)
        hturn(3)
        hcopy(2, "S")
        smax(0)
        hcopy(3, "S")
        hquant(2, 2)
        smax(1)
        sexp(0)
        spread_mm("g", eights, g_row)
        spread_copy("g", g_b)
        score(3, 3)
        score(2, 1)
        score(2, 2)
        sexp(1)
        srec(0)
        score(3, 0)
        score(3, 2)
        score(3, 1)
        zmm(1)
        zmax(1, 0)
        zmax(1, 1)
        score(2, 3)
        zneg(1)
        score(2, 0)
        smax(3)
        zexp(1)
        smax(2)
        srec(1)
        zmm(0)
        zmax(0, 1)
        zmax(0, 0)
        gain(0, 0)
        sexp(3)
        turn(0, 0)
        gn1()
        zneg(0)
        sexp(2)
        gain(0, 1)
        zexp(0)
        gain(1, 0)
        zmm(2)
        turn(0, 1)
        zmax(2, 0)
        zmax(2, 1)
        g1()
        g2()
        zneg(2)
        tcopy(0, 0)
        tcopy(0, 1)
        turn(1, 0)
        srec(2)
        gn2()
        aquant(0)
        zexp(2)
        gain(1, 1)
        g3()
        tcopy(1, 0)
        zmm(3)
        turn(1, 1)
        gn3()
        zmax(3, 0)
        kmm(0, 0)
        zmax(3, 1)
        srec(3)
        g4()
        kmm(0, 2)
        zneg(3)
        zsum(0)
        g5()
        zsum(1)
        zsum(2)
        tcopy(1, 1)
        g6()
        aquant(1)
        zexp(3)
        g6b()
        kmm(0, 4)
        zinv(1)
        zinv(2)
        g6c()
        zinv(0)
        g6d()
        kmm(0, 1)
        g7()
        zc1(0)
        yaff(0)
        zc1(1)
        gain(2, 1)
        gain(2, 0)
        kmm(1, 2)
        turn(2, 1)
        zsum(3)
        tcopy(2, 1)
        mix(0, 0)
        gain(3, 1)
        turn(2, 0)
        kmm(1, 4)
        gain(3, 0)
        tcopy(2, 0)
        mix(0, 2)
        mix(0, 4)
        kmm(1, 0)
        turn(3, 1)
        aquant(2)
        turn(3, 0)
        zc1(2)
        kmm(0, 3)
        yaff(1)
        mix(1, 4)
        zinv(3)
        mix(0, 1)
        mix(1, 2)
        tcopy(3, 1)
        tcopy(3, 0)
        kmm(2, 2)
        zc1(3)
        kmm(2, 0)
        aquant(3)
        mix(1, 0)
        yaff(2)
        yaff(3)
        mix(2, 0)
        kmm(2, 4)
        mix(0, 3)
        kmm(3, 2)
        kmm(3, 4)
        mix(2, 2)
        mix(2, 4)
        mix(3, 2)
        mix(3, 4)
        kmm(3, 0)
        plane_copy(4, [("S", 88), ("V", 168)])
        kmm(3, 1)
        mix(3, 0)
        plane_copy(2, [("S", 408), ("V", 104)])
        plane_quant(4)
        mix(3, 1)
        plane_copy(0, [("S", 408), ("V", 104)])
        plane_quant(2)
        kmm(2, 1)
        kmm(1, 1)
        kmm(2, 3)
        mix(2, 1)
        mix(1, 1)
        mix(2, 3)
        kmm(1, 3)
        kmm(3, 3)
        plane_quant(0)
        mix(1, 3)
        mix(3, 3)
        plane_copy(1, [("S", 408), ("V", 104)])
        plane_copy(3, [("S", 88), ("V", 168)])
        plane_quant(1)
        plane_quant(3)
        for q in range(4):
            nc.sync.dma_start(
                out=out_2[0, 4 * q : 4 * q + 4, :].bitcast(I32), in_=oqs[32 * q : 32 * q + 4, :].bitcast(I32)
            )
